import numpy as np
import ml_dtypes


def mxq(x, axis, fmt="e4m3"):
    dtype, down = {"e4m3": (ml_dtypes.float8_e4m3fn, 7), "e5m2": (ml_dtypes.float8_e5m2, 14)}[fmt]
    v = np.moveaxis(np.asarray(x, np.float32).astype(ml_dtypes.bfloat16).astype(np.float64), axis, -1)
    blocks = v.reshape(v.shape[:-1] + (-1, 32))
    amax = np.abs(blocks).max(-1, keepdims=True)
    byte = np.maximum(np.where(amax > 0, np.frexp(amax)[1] - 1 + 127, 0) - down, 1)
    scale = np.exp2(byte - 127.0)
    codes = (blocks / scale).astype(np.float32).astype(dtype).astype(np.float64)
    return np.moveaxis((codes * scale).reshape(v.shape), -1, axis)


WIDE = False


def mx_kscale(k):
    if not WIDE:
        return np.ones(k)
    levels = np.array([10, -10, 5, -5, 0])
    if k % 512:
        return np.exp2(np.random.permutation(np.resize(levels, k // 32))).repeat(32)
    a = np.empty((k // 512, 16))
    for p in range(k // 512):
        a[p, :8] = np.random.permutation(np.resize(levels, 8))
        for g in range(8):
            far = levels[np.abs(levels - a[p, g]) >= 10]
            a[p, g + 8] = far[np.random.randint(len(far))]
    return np.exp2(a.ravel()).repeat(32)


def f64(x):
    return np.asarray(x).astype(np.float64)


def striped(idx):
    return np.tile(idx.reshape(-1, 16).T, (8, 1)).astype(np.uint16)


def unstriped(offs):
    return offs[:16].T.reshape(-1).astype(np.int64)


E2M1 = np.array([0.0, 0.5, 1.0, 1.5, 2.0, 3.0, 4.0, 6.0, -0.0, -0.5, -1.0, -1.5, -2.0, -3.0, -4.0, -6.0])


def pack_weight(w, fmt):
    k, n = w.shape
    w = f64(np.asarray(w, np.float32).astype(ml_dtypes.bfloat16)).reshape(k // 32, 32, n)
    amax = np.abs(w).max(1)
    if fmt == "e4m3":
        byte = np.frexp(amax)[1] - 1 + 127 - 7
    else:
        mant, ex = np.frexp(amax / 6.0)
        byte = np.where(mant > 0.5, ex, ex - 1) + 127
    byte = np.clip(np.where(amax > 0, byte, 1), 1, 254)
    scaled = (w * np.exp2(127.0 - byte)[:, None, :]).reshape(k, n).astype(np.float32)
    by_word = np.ascontiguousarray(scaled.reshape(k // 512, 128, 4, n).transpose(0, 1, 3, 2))
    if fmt == "e4m3":
        words = by_word.astype(ml_dtypes.float8_e4m3fn).view(np.uint8)
    else:
        c = by_word.astype(ml_dtypes.float4_e2m1fn).view(np.uint8) & 0xF
        words = (c[..., 0::2] | (c[..., 1::2] << 4)).reshape(k // 512, 128, 2 * n)
    return np.ascontiguousarray(words), np.ascontiguousarray(byte.astype(np.uint8).reshape(k // 512, 16, n))


def unpack_weight(words, scales, fmt):
    g, _, n = scales.shape
    words = np.ascontiguousarray(words).reshape(g, 128, n, -1)
    if fmt == "e4m3":
        vals = words.view(ml_dtypes.float8_e4m3fn).astype(np.float64)
    else:
        nib = np.empty((g, 128, n, 4), np.uint8)
        nib[..., 0::2] = words & 0xF
        nib[..., 1::2] = words >> 4
        vals = E2M1[nib]
    vals = vals * np.repeat(np.exp2(scales.astype(np.float64) - 127.0), 8, axis=1)[..., None]
    return vals.transpose(0, 1, 3, 2).reshape(g * 512, n)


def gelu(v):
    return 0.5 * v * (1.0 + np.tanh(np.sqrt(2.0 / np.pi) * (v + 0.044715 * v**3)))


K, T, S, H, P = 1024, 4096, 1024, 1024, 512

def setup_inputs():
    n = np.random.standard_normal
    s = mx_kscale(K)[:, None]
    u = mx_kscale(H)[:, None]
    tab_words, tab_scales = pack_weight(n((K, T)) * s, "e4m3")
    w4_words, w4_scales = pack_weight(1.4 * n((K, H)) / np.sqrt(K) / s, "e2m1")
    gain = np.exp(0.3 * n(H)) * u[:, 0]
    w2 = 1.6 * n((H, H)) / np.sqrt(H) / u
    d = 0.7 * n(H)
    skip = np.exp(0.3 * n(H)) / u[:, 0]
    wgo = np.exp(0.3 * n((128, P)))
    return {
        "tab_words": tab_words, "tab_scales": tab_scales,
        "offs": striped(np.random.permutation(T)[:S]),
        "pos1": striped(np.random.permutation(S)[:P]),
        "w4_words": w4_words, "w4_scales": w4_scales,
        "gain": gain.astype(np.float32),
        "w2": w2.astype(np.float32),
        "d": d.astype(np.float32),
        "skip": skip.astype(np.float32),
        "wgo": wgo.astype(np.float32),
    }

def reference(tab_words, tab_scales, offs, pos1, w4_words, w4_scales, gain, w2, d, skip, wgo):
    v = unpack_weight(tab_words, tab_scales, "e4m3")[:, unstriped(offs)]
    w4 = unpack_weight(w4_words, w4_scales, "e2m1")
    h = f64(gain)[:, None] * np.tanh(w4.T @ v)
    x = mxq(h[:, unstriped(pos1)], 0, "e4m3")
    w2q = mxq(f64(w2), 0, "e4m3")
    y = np.tanh((w2q.T @ x) + f64(d)[:, None])
    out = f64(skip)[:, None] * h
    out[:, unstriped(pos1)] = np.tile(f64(wgo), (H // 128, 1)) * y
    return out

@@ -1,0 +1,254 @@
+from contextlib import ExitStack
+
+import concourse.mybir as mybir
+
+K, T, S, H, M2 = 1024, 4096, 1024, 1024, 512
+FLOPS = 2 * K * H * S + 2 * H * H * M2
+
+F32 = mybir.dt.float32
+BF16 = mybir.dt.bfloat16
+I32 = mybir.dt.int32
+U32 = mybir.dt.uint32
+U16 = mybir.dt.uint16
+U8 = mybir.dt.uint8
+FP8X4 = mybir.dt.float8_e4m3fn_x4
+FP4X4 = mybir.dt.float4_e2m1fn_x4
+MULT = mybir.AluOpType.mult
+TANH = mybir.ActivationFunctionType.Tanh
+COPY = mybir.ActivationFunctionType.Copy
+
+P = 128
+PACK = 4
+PASSES = 2
+BANK = 512
+TILES = H // P
+BANKS = 8
+HALF = M2 // 2
+
+
+def tile_list_tarnish_patch_features_kernel(
+    tc, tab_words, tab_scales, offs, pos1, w4_words, w4_scales, gain, w2, d, skip, wgo, out
+):
+    nc = tc.nc
+    with ExitStack() as ctx:
+        lists = ctx.enter_context(tc.tile_pool(name="lists", bufs=1))
+        held = ctx.enter_context(tc.tile_pool(name="held", bufs=1))
+        ring = ctx.enter_context(tc.tile_pool(name="ring", bufs=2))
+        ys = ctx.enter_context(tc.tile_pool(name="ys", bufs=3))
+        psum = ctx.enter_context(tc.psum_pool(name="psum", bufs=BANKS))
+
+        offs_t = lists.tile([P, S // 16], U16, name="offs_t")
+        pos_t = lists.tile([P, M2 // 16], U16, name="pos_t")
+        nc.sync.dma_start(offs_t[:], offs)
+
+        tab_sc = held.tile([P, T], U8, name="tab_sc", align_bytes=64)
+        w4_sc = held.tile([P, H], U8, name="w4_sc", tag="spread", align_bytes=64)
+        planes = held.tile([P, PASSES, S + H], U8, name="planes", align_bytes=64)
+        nc.vector.memset(tab_sc[:].bitcast(I32), 0)
+        nc.vector.memset(w4_sc[:].bitcast(I32), 0)
+        nc.vector.memset(planes[:].bitcast(I32), 0)
+        w4_raw = held.tile([P, PASSES, H // 2], I32, name="w4_raw", align_bytes=64)
+        nc.sync.dma_start(w4_raw[:], w4_words.rearrange("a p c -> p a c").bitcast(I32))
+        nc.sync.dma_start(tab_sc[0:P:4, :].bitcast(I32), tab_scales.rearrange("a q t -> q a t").bitcast(I32))
+        nc.sync.dma_start(w4_sc[0:P:4, :].bitcast(I32), w4_scales.rearrange("a q c -> q a c").bitcast(I32))
+        nc.sync.dma_start(pos_t[:], pos1)
+        table = []
+        for a in range(PASSES):
+            tab = held.tile([P, T], I32, name=f"table{a}", tag=f"big{a}", align_bytes=64)
+            nc.sync.dma_start(tab[:], tab_words[a].rearrange("p t i -> p (t i)").bitcast(I32))
+            table.append(tab)
+
+        vecs = {}
+        for name, vec in (("gain", gain), ("skip", skip), ("d", d)):
+            vt = held.tile([P, PASSES, PACK], F32, name=f"{name}_t")
+            nc.gpsimd.dma_start(vt[:], vec.rearrange("(b p t) -> p b t", b=PASSES, t=PACK))
+            vecs[name] = vt[:].rearrange("p b t -> p (b t)")
+
+        v_sc = held.tile([P, S], U8, name="v_sc", align_bytes=64)
+        nc.vector.tensor_copy(v_sc[:], tab_sc[:].indirect(offs_t[:]))
+        rows = held.tile([P, S + H], U8, name="rows", align_bytes=64)
+        nc.vector.tensor_copy(
+            rows[:, S:].rearrange("p (b t q) -> p b t q", b=PASSES, t=PACK),
+            w4_sc[:].rearrange("p (b q t) -> p b t q", b=PASSES, t=PACK),
+        )
+        nc.vector.tensor_copy(rows[:, :S].bitcast(I32), v_sc[:].bitcast(I32))
+        for quad in range(4):
+            nc.scalar.dma_start(
+                planes[32 * quad : 32 * quad + 4, :, :].bitcast(I32),
+                rows[32 * quad : 32 * quad + 32 : 4, :].bitcast(I32),
+            )
+
+        w4_dealt = held.tile([P, PASSES * H * 2], U8, name="w4_dealt", tag="w4_wgo", align_bytes=64)
+        nc.vector.tensor_copy(
+            w4_dealt[:].bitcast(U16).rearrange("p (g t q) -> p g t q", t=PACK, q=P),
+            w4_raw[:].rearrange("p a c -> p (a c)").bitcast(U16).rearrange("p (g q t) -> p g t q", t=PACK, q=P),
+        )
+        page_scale = held.tile([P, TILES], F32, name="page_scale")
+        nc.gpsimd.tensor_tensor(page_scale[:], vecs["gain"], vecs["skip"], MULT)
+
+        spread = held.tile([P, PACK * (M2 + HALF)], F32, name="spread", tag="spread", align_bytes=64)
+        gain0 = spread[:, : PACK * M2].rearrange("p (t m) -> p t m", t=PACK)
+        gain1 = spread[:, PACK * M2 :].rearrange("p (t m) -> p t m", t=PACK)
+        nc.vector.tensor_copy(gain0, vecs["gain"][:, :PACK].unsqueeze(2).to_broadcast([P, PACK, M2]))
+        nc.vector.tensor_copy(gain1, vecs["gain"][:, PACK:].unsqueeze(2).to_broadcast([P, PACK, HALF]))
+
+        v_words = [held.tile([P, S], U32, name=f"v_words{a}", align_bytes=64) for a in range(PASSES)]
+        nc.vector.tensor_copy(v_words[0][:], table[0][:].bitcast(U32).indirect(offs_t[:]))
+
+        groups = [(0, 0), (1, 0), (0, 1), (1, 1)] + [(k, s) for k in range(2, TILES) for s in range(2)]
+
+        def first_stage_pass(acc, k, s, a):
+            cols = slice(s * BANK, (s + 1) * BANK)
+            nc.tensor.matmul_mx(
+                acc[:],
+                lhsT=w4_dealt[:, 2 * (a * H + k * P) : 2 * (a * H + (k + 1) * P)].bitcast(FP4X4),
+                lhsT_scale=planes[:, a, S + k * P : S + (k + 1) * P],
+                rhs=v_words[a][:, cols].bitcast(FP8X4),
+                rhs_scale=planes[:, a, cols],
+                start=(a == 0),
+                stop=(a == PASSES - 1),
+            )
+
+        accs = {}
+        for k, s in groups[:BANKS]:
+            accs[k, s] = psum.tile([P, BANK], F32, name="acc")
+            first_stage_pass(accs[k, s], k, s, 0)
+        for s in range(2):
+            nc.vector.tensor_copy(
+                v_words[1][:, s * BANK : (s + 1) * BANK],
+                table[1][:].bitcast(U32).indirect(offs_t[:, s * 32 : (s + 1) * 32]),
+            )
+
+        w2_raw = []
+        w2_rows = w2.rearrange("(b p j) n -> b p j n", b=PASSES, j=PACK)
+        for c in range(2):
+            raw = held.tile([P, PASSES, PACK, BANK], F32, name=f"w2_raw{c}", tag=f"big{c}", align_bytes=64)
+            for b in range(PASSES):
+                nc.sync.dma_start(raw[:, b, :, :], w2_rows[b][:, :, c * BANK : (c + 1) * BANK])
+            w2_raw.append(raw)
+
+        tanhs = [held.tile([P, S], F32, name=f"tanh{k}") for k in range(TILES)]
+        x_codes = [held.tile([P, M2], U32, name=f"x_codes{b}", align_bytes=64) for b in range(PASSES)]
+        x_scales = [held.tile([P, M2], U8, name=f"x_scales{b}", align_bytes=64) for b in range(PASSES)]
+
+        def weave(picked, width, name):
+            woven = held.tile([P, width, PACK], BF16, name=name, align_bytes=64)
+            nc.vector.tensor_copy(
+                woven[:].rearrange("p (c i) t -> p c t i", i=4),
+                picked[:].rearrange("p t (c i) -> p c t i", i=4),
+            )
+            return woven
+
+        def quantise_x(woven, b, cols):
+            nc.vector.quantize_mx(
+                x_codes[b][:, cols].bitcast(FP8X4),
+                x_scales[b][:, cols],
+                woven[:].rearrange("p m t -> p (m t)"),
+            )
+
+        picked0 = held.tile([P, PACK, M2], F32, name="picked0")
+        picked1 = held.tile([P, PACK, HALF], F32, name="picked1a")
+        woven0 = None
+        for k, s in groups:
+            if (k, s) not in accs:
+                accs[k, s] = psum.tile([P, BANK], F32, name="acc")
+                first_stage_pass(accs[k, s], k, s, 0)
+            first_stage_pass(accs[k, s], k, s, 1)
+            nc.scalar.activation(tanhs[k][:, s * BANK : (s + 1) * BANK], accs[k, s][:], TANH)
+            if s == 1:
+                if k < PACK:
+                    nc.vector.tensor_tensor(picked0[:, k, :], tanhs[k][:].indirect(pos_t[:]), gain0[:, k, :], MULT)
+                else:
+                    nc.vector.tensor_tensor(
+                        picked1[:, k - PACK, :], tanhs[k][:].indirect(pos_t[:, 0:16]), gain1[:, k - PACK, :], MULT
+                    )
+                if k == PACK - 1:
+                    woven0 = weave(picked0, M2, "woven0")
+                if k == PACK:
+                    quantise_x(woven0, 0, slice(0, M2))
+
+        wgo_t = held.tile([P, PACK, M2], F32, name="wgo_t", tag="w4_wgo", align_bytes=64)
+        for quad in range(4):
+            nc.sync.dma_start(wgo_t[32 * quad : 32 * quad + 32, :, :], wgo.rearrange("(v t) m -> v t m", t=PACK))
+
+        def round_w2(pair):
+            c, t0 = pair // 2, 2 * (pair % 2)
+            tag = "first" if pair == 0 else f"rounded{pair}"
+            rounded = held.tile([P, PASSES, 2, P, PACK], BF16, name=f"w2_rounded{pair}", tag=tag, align_bytes=64)
+            for b in range(PASSES):
+                nc.scalar.copy(
+                    rounded[:, b, :, :, :].rearrange("p t q j -> p q j t"),
+                    w2_raw[c][:, b, :, :].rearrange("p j (q t) -> p q j t", t=PACK)[:, :, :, t0 : t0 + 2],
+                )
+            return rounded
+
+        def quantise_w2(rounded):
+            codes = ring.tile([P, PASSES, 2, P], U32, name="w2_codes", align_bytes=64)
+            scales = ring.tile([P, PASSES, 2, P], U8, name="w2_scales", align_bytes=64)
+            nc.vector.quantize_mx(
+                codes[:].rearrange("p b t q -> p (b t q)").bitcast(FP8X4),
+                scales[:].rearrange("p b t q -> p (b t q)"),
+                rounded[:].rearrange("p b t q j -> p (b t q j)"),
+            )
+            return codes, scales
+
+        def second_stage(k, weights, y, cols):
+            codes, scales = weights
+            width = cols.stop - cols.start
+            acc = psum.tile([P, BANK], F32, name="acc")
+            for b in range(PASSES):
+                nc.tensor.matmul_mx(
+                    acc[:, :width],
+                    lhsT=codes[:, b, k % 2, :].bitcast(FP8X4),
+                    lhsT_scale=scales[:, b, k % 2, :],
+                    rhs=x_codes[b][:, cols].bitcast(FP8X4),
+                    rhs_scale=x_scales[b][:, cols],
+                    start=(b == 0),
+                    stop=(b == PASSES - 1),
+                )
+            nc.scalar.activation(y[:, cols], acc[:, :width], TANH, bias=vecs["d"][:, k : k + 1])
+
+        def make_page(k):
+            page = held.tile([P, S], F32, name=f"page{k}")
+            nc.scalar.activation(page[:], tanhs[k][:], COPY, scale=page_scale[:, k : k + 1])
+            return page
+
+        def put(k, page, y, cols):
+            offsets = pos_t[:, cols.start // 16 : cols.stop // 16]
+            nc.vector.tensor_tensor(page[:].indirect(offsets), y[:, cols], wgo_t[:, k % PACK, cols], MULT)
+
+        out_rows = out.rearrange("(b p t) j -> b t p j", b=PASSES, t=PACK)
+        halves = [slice(0, HALF), slice(HALF, M2)]
+
+        rounded = round_w2(0)
+        woven1a = weave(picked1, HALF, "woven1a")
+        weights = quantise_w2(rounded)
+        quantise_x(woven1a, 1, halves[0])
+        page = make_page(0)
+        y = ys.tile([P, M2], F32, name="y")
+        second_stage(0, weights, y, halves[0])
+        rounded = round_w2(1)
+
+        picked1 = held.tile([P, PACK, HALF], F32, name="picked1b", tag="first", align_bytes=64)
+        for t in range(PACK):
+            nc.vector.tensor_tensor(
+                picked1[:, t, :], tanhs[PACK + t][:].indirect(pos_t[:, 16:32]), gain1[:, t, :], MULT
+            )
+        woven1b = weave(picked1, HALF, "woven1b")
+        quantise_x(woven1b, 1, halves[1])
+        put(0, page, y, halves[0])
+        second_stage(0, weights, y, halves[1])
+        next_weights = quantise_w2(rounded)
+        put(0, page, y, halves[1])
+        nc.sync.dma_start(out_rows[0][0], page[:])
+
+        for k in range(1, TILES):
+            if k % 2 == 0:
+                weights = next_weights
+            page = make_page(k)
+            y = ys.tile([P, M2], F32, name="y")
+            second_stage(k, weights, y, slice(0, M2))
+            put(k, page, y, slice(0, M2))
+            nc.sync.dma_start(out_rows[k // PACK][k % PACK], page[:])
+            if k % 2 == 0 and k + 2 < TILES:
+                next_weights = quantise_w2(round_w2(k // 2 + 1))

@@ -41,22 +41,29 @@ def tile_list_tarnish_patch_features_kernel(
         pos_t = lists.tile([P, M2 // 16], U16, name="pos_t")
         nc.sync.dma_start(offs_t[:], offs)
 
-        tab_sc = held.tile([P, T], U8, name="tab_sc", align_bytes=64)
-        w4_sc = held.tile([P, H], U8, name="w4_sc", tag="spread", align_bytes=64)
+        w4_sc = held.tile([P, H], U8, name="w4_sc", align_bytes=64)
+        tab_sc = held.tile([P, T], U8, name="tab_sc", tag="early", align_bytes=64)
         planes = held.tile([P, PASSES, S + H], U8, name="planes", align_bytes=64)
-        nc.vector.memset(tab_sc[:].bitcast(I32), 0)
-        nc.vector.memset(w4_sc[:].bitcast(I32), 0)
+        for lo, hi in ((32, 64), (64, P)):
+            nc.vector.memset(w4_sc[lo:hi, :].bitcast(I32), 0)
+            nc.vector.memset(tab_sc[lo:hi, :].bitcast(I32), 0)
         nc.vector.memset(planes[:].bitcast(I32), 0)
-        w4_raw = held.tile([P, PASSES, H // 2], I32, name="w4_raw", align_bytes=64)
-        nc.sync.dma_start(w4_raw[:], w4_words.rearrange("a p c -> p a c").bitcast(I32))
-        nc.sync.dma_start(tab_sc[0:P:4, :].bitcast(I32), tab_scales.rearrange("a q t -> q a t").bitcast(I32))
-        nc.sync.dma_start(w4_sc[0:P:4, :].bitcast(I32), w4_scales.rearrange("a q c -> q a c").bitcast(I32))
-        nc.sync.dma_start(pos_t[:], pos1)
+        w4_cols = w4_words.rearrange("a p (b c) -> b p a c", b=PASSES)
+        w4_raw = [held.tile([P, PASSES, BANK // 2], I32, name=f"w4_raw{b}", align_bytes=64) for b in range(PASSES)]
+        nc.sync.dma_start(w4_sc[0:32, :].bitcast(I32), w4_scales.rearrange("a q c -> q a c").bitcast(I32))
+        nc.sync.dma_start(tab_sc[0:32, :].bitcast(I32), tab_scales.rearrange("a q t -> q a t").bitcast(I32))
         table = []
-        for a in range(PASSES):
+
+        def load_table(a):
             tab = held.tile([P, T], I32, name=f"table{a}", tag=f"big{a}", align_bytes=64)
             nc.sync.dma_start(tab[:], tab_words[a].rearrange("p t i -> p (t i)").bitcast(I32))
             table.append(tab)
+
+        nc.sync.dma_start(w4_raw[0][:], w4_cols[0].bitcast(I32))
+        load_table(0)
+        nc.sync.dma_start(pos_t[:], pos1)
+        load_table(1)
+        nc.sync.dma_start(w4_raw[1][:], w4_cols[1].bitcast(I32))
 
         vecs = {}
         for name, vec in (("gain", gain), ("skip", skip), ("d", d)):
@@ -64,25 +71,31 @@ def tile_list_tarnish_patch_features_kernel(
             nc.gpsimd.dma_start(vt[:], vec.rearrange("(b p t) -> p b t", b=PASSES, t=PACK))
             vecs[name] = vt[:].rearrange("p b t -> p (b t)")
 
-        v_sc = held.tile([P, S], U8, name="v_sc", align_bytes=64)
-        nc.vector.tensor_copy(v_sc[:], tab_sc[:].indirect(offs_t[:]))
-        rows = held.tile([P, S + H], U8, name="rows", align_bytes=64)
+        rows = held.tile([P, S + H], U8, name="rows", tag="spread", align_bytes=64)
         nc.vector.tensor_copy(
             rows[:, S:].rearrange("p (b t q) -> p b t q", b=PASSES, t=PACK),
             w4_sc[:].rearrange("p (b q t) -> p b t q", b=PASSES, t=PACK),
         )
+        v_sc = held.tile([P, S], U8, name="v_sc", align_bytes=64)
+        nc.vector.tensor_copy(v_sc[:], tab_sc[:].indirect(offs_t[:]))
         nc.vector.tensor_copy(rows[:, :S].bitcast(I32), v_sc[:].bitcast(I32))
         for quad in range(4):
             nc.scalar.dma_start(
                 planes[32 * quad : 32 * quad + 4, :, :].bitcast(I32),
-                rows[32 * quad : 32 * quad + 32 : 4, :].bitcast(I32),
+                rows[8 * quad : 8 * quad + 8, :].bitcast(I32),
             )
 
-        w4_dealt = held.tile([P, PASSES * H * 2], U8, name="w4_dealt", tag="w4_wgo", align_bytes=64)
-        nc.vector.tensor_copy(
-            w4_dealt[:].bitcast(U16).rearrange("p (g t q) -> p g t q", t=PACK, q=P),
-            w4_raw[:].rearrange("p a c -> p (a c)").bitcast(U16).rearrange("p (g q t) -> p g t q", t=PACK, q=P),
-        )
+        w4_dealt = []
+
+        def deal_w4(b, tag):
+            dealt = held.tile([P, PASSES * BANK * 2], U8, name=f"w4_dealt{b}", tag=tag, align_bytes=64)
+            nc.vector.tensor_copy(
+                dealt[:].bitcast(U16).rearrange("p (a t q) -> p a t q", t=PACK, q=P),
+                w4_raw[b][:].rearrange("p a c -> p (a c)").bitcast(U16).rearrange("p (a q t) -> p a t q", t=PACK, q=P),
+            )
+            w4_dealt.append(dealt)
+
+        deal_w4(0, "early")
         page_scale = held.tile([P, TILES], F32, name="page_scale")
         nc.gpsimd.tensor_tensor(page_scale[:], vecs["gain"], vecs["skip"], MULT)
 
@@ -99,9 +112,10 @@ def tile_list_tarnish_patch_features_kernel(
 
         def first_stage_pass(acc, k, s, a):
             cols = slice(s * BANK, (s + 1) * BANK)
+            first = a * BANK + (k % PACK) * P
             nc.tensor.matmul_mx(
                 acc[:],
-                lhsT=w4_dealt[:, 2 * (a * H + k * P) : 2 * (a * H + (k + 1) * P)].bitcast(FP4X4),
+                lhsT=w4_dealt[k // PACK][:, 2 * first : 2 * (first + P)].bitcast(FP4X4),
                 lhsT_scale=planes[:, a, S + k * P : S + (k + 1) * P],
                 rhs=v_words[a][:, cols].bitcast(FP8X4),
                 rhs_scale=planes[:, a, cols],
@@ -119,6 +133,8 @@ def tile_list_tarnish_patch_features_kernel(
                 table[1][:].bitcast(U32).indirect(offs_t[:, s * 32 : (s + 1) * 32]),
             )
 
+        deal_w4(1, "w4_wgo")
+
         w2_raw = []
         w2_rows = w2.rearrange("(b p j) n -> b p j n", b=PASSES, j=PACK)
         for c in range(2):
@@ -131,7 +147,7 @@ def tile_list_tarnish_patch_features_kernel(
         x_codes = [held.tile([P, M2], U32, name=f"x_codes{b}", align_bytes=64) for b in range(PASSES)]
         x_scales = [held.tile([P, M2], U8, name=f"x_scales{b}", align_bytes=64) for b in range(PASSES)]
 
-        def weave(picked, width, name):
+        def weave(picked, b, width, name):
             woven = held.tile([P, width, PACK], BF16, name=name, align_bytes=64)
             nc.vector.tensor_copy(
                 woven[:].rearrange("p (c i) t -> p c t i", i=4),
@@ -163,7 +179,7 @@ def tile_list_tarnish_patch_features_kernel(
                         picked1[:, k - PACK, :], tanhs[k][:].indirect(pos_t[:, 0:16]), gain1[:, k - PACK, :], MULT
                     )
                 if k == PACK - 1:
-                    woven0 = weave(picked0, M2, "woven0")
+                    woven0 = weave(picked0, 0, M2, "woven0")
                 if k == PACK:
                     quantise_x(woven0, 0, slice(0, M2))
 
@@ -221,7 +237,7 @@ def tile_list_tarnish_patch_features_kernel(
         halves = [slice(0, HALF), slice(HALF, M2)]
 
         rounded = round_w2(0)
-        woven1a = weave(picked1, HALF, "woven1a")
+        woven1a = weave(picked1, 1, HALF, "woven1a")
         weights = quantise_w2(rounded)
         quantise_x(woven1a, 1, halves[0])
         page = make_page(0)
@@ -234,7 +250,7 @@ def tile_list_tarnish_patch_features_kernel(
             nc.vector.tensor_tensor(
                 picked1[:, t, :], tanhs[PACK + t][:].indirect(pos_t[:, 16:32]), gain1[:, t, :], MULT
             )
-        woven1b = weave(picked1, HALF, "woven1b")
+        woven1b = weave(picked1, 1, HALF, "woven1b")
         quantise_x(woven1b, 1, halves[1])
         put(0, page, y, halves[0])
         second_stage(0, weights, y, halves[1])

@@ -22,7 +22,7 @@ PACK = 4
 PASSES = 2
 BANK = 512
 TILES = H // P
-BANKS = 8
+BANKS = 4
 HALF = M2 // 2
 
 
@@ -49,20 +49,23 @@ def tile_list_tarnish_patch_features_kernel(
             nc.vector.memset(tab_sc[lo:hi, :].bitcast(I32), 0)
         nc.vector.memset(planes[:].bitcast(I32), 0)
         w4_cols = w4_words.rearrange("a p (b c) -> b p a c", b=PASSES)
-        w4_raw = [held.tile([P, PASSES, BANK // 2], I32, name=f"w4_raw{b}", align_bytes=64) for b in range(PASSES)]
+        w4_raw = [
+            held.tile([P, PASSES, BANK // 2], I32, name=f"w4_raw{b}", tag=f"raw{b}", align_bytes=64)
+            for b in range(PASSES)
+        ]
         nc.sync.dma_start(w4_sc[0:32, :].bitcast(I32), w4_scales.rearrange("a q c -> q a c").bitcast(I32))
         nc.sync.dma_start(tab_sc[0:32, :].bitcast(I32), tab_scales.rearrange("a q t -> q a t").bitcast(I32))
         table = []
 
-        def load_table(a):
+        def load_table(a, piece):
             tab = held.tile([P, T], I32, name=f"table{a}", tag=f"big{a}", align_bytes=64)
-            nc.sync.dma_start(tab[:], tab_words[a].rearrange("p t i -> p (t i)").bitcast(I32))
+            nc.sync.dma_start(tab[:], tab_words[a].rearrange("p t i -> p (t i)").bitcast(I32), max_dma_last_dim=piece)
             table.append(tab)
 
         nc.sync.dma_start(w4_raw[0][:], w4_cols[0].bitcast(I32))
-        load_table(0)
+        load_table(0, 4 * T)
         nc.sync.dma_start(pos_t[:], pos1)
-        load_table(1)
+        load_table(1, T)
         nc.sync.dma_start(w4_raw[1][:], w4_cols[1].bitcast(I32))
 
         vecs = {}
@@ -71,7 +74,7 @@ def tile_list_tarnish_patch_features_kernel(
             nc.gpsimd.dma_start(vt[:], vec.rearrange("(b p t) -> p b t", b=PASSES, t=PACK))
             vecs[name] = vt[:].rearrange("p b t -> p (b t)")
 
-        rows = held.tile([P, S + H], U8, name="rows", tag="spread", align_bytes=64)
+        rows = held.tile([P, S + H], U8, name="rows", align_bytes=64)
         nc.vector.tensor_copy(
             rows[:, S:].rearrange("p (b t q) -> p b t q", b=PASSES, t=PACK),
             w4_sc[:].rearrange("p (b q t) -> p b t q", b=PASSES, t=PACK),
@@ -99,11 +102,8 @@ def tile_list_tarnish_patch_features_kernel(
         page_scale = held.tile([P, TILES], F32, name="page_scale")
         nc.gpsimd.tensor_tensor(page_scale[:], vecs["gain"], vecs["skip"], MULT)
 
-        spread = held.tile([P, PACK * (M2 + HALF)], F32, name="spread", tag="spread", align_bytes=64)
-        gain0 = spread[:, : PACK * M2].rearrange("p (t m) -> p t m", t=PACK)
-        gain1 = spread[:, PACK * M2 :].rearrange("p (t m) -> p t m", t=PACK)
-        nc.vector.tensor_copy(gain0, vecs["gain"][:, :PACK].unsqueeze(2).to_broadcast([P, PACK, M2]))
-        nc.vector.tensor_copy(gain1, vecs["gain"][:, PACK:].unsqueeze(2).to_broadcast([P, PACK, HALF]))
+        gains = held.tile([P, TILES, M2], F32, name="gains", tag="raw0", align_bytes=64)
+        nc.vector.tensor_copy(gains[:], vecs["gain"].unsqueeze(2).to_broadcast([P, TILES, M2]))
 
         v_words = [held.tile([P, S], U32, name=f"v_words{a}", align_bytes=64) for a in range(PASSES)]
         nc.vector.tensor_copy(v_words[0][:], table[0][:].bitcast(U32).indirect(offs_t[:]))
@@ -147,24 +147,35 @@ def tile_list_tarnish_patch_features_kernel(
         x_codes = [held.tile([P, M2], U32, name=f"x_codes{b}", align_bytes=64) for b in range(PASSES)]
         x_scales = [held.tile([P, M2], U8, name=f"x_scales{b}", align_bytes=64) for b in range(PASSES)]
 
-        def weave(picked, b, width, name):
-            woven = held.tile([P, width, PACK], BF16, name=name, align_bytes=64)
-            nc.vector.tensor_copy(
+        def weave(copy, b, half):
+            woven = held.tile([P, HALF, PACK], BF16, name=f"woven{b}{half}", align_bytes=64)
+            copy(
                 woven[:].rearrange("p (c i) t -> p c t i", i=4),
-                picked[:].rearrange("p t (c i) -> p c t i", i=4),
+                picked[b][:, :, halves[half]].rearrange("p t (c i) -> p c t i", i=4),
             )
             return woven
 
-        def quantise_x(woven, b, cols):
+        def quantise_x(woven, b, half):
+            cols = halves[half]
             nc.vector.quantize_mx(
                 x_codes[b][:, cols].bitcast(FP8X4),
                 x_scales[b][:, cols],
                 woven[:].rearrange("p m t -> p (m t)"),
             )
 
-        picked0 = held.tile([P, PACK, M2], F32, name="picked0")
-        picked1 = held.tile([P, PACK, HALF], F32, name="picked1a")
-        woven0 = None
+        halves = [slice(0, HALF), slice(HALF, M2)]
+        picked0 = held.tile([P, PACK * M2], F32, name="picked0")
+        shared = held.tile([P, PACK * M2 + 3 * HALF], F32, name="shared", align_bytes=64)
+        picked = [flat.rearrange("p (t m) -> p t m", t=PACK) for flat in (picked0[:], shared[:, : PACK * M2])]
+        first_rounded = shared[:, PACK * M2 - HALF :].bitcast(BF16)
+
+        def pick(k, cols):
+            offsets = pos_t[:, cols.start // 16 : cols.stop // 16]
+            nc.vector.tensor_tensor(
+                picked[k // PACK][:, k % PACK, cols], tanhs[k][:].indirect(offsets), gains[:, k, cols], MULT
+            )
+
+        woven = None
         for k, s in groups:
             if (k, s) not in accs:
                 accs[k, s] = psum.tile([P, BANK], F32, name="acc")
@@ -172,16 +183,11 @@ def tile_list_tarnish_patch_features_kernel(
             first_stage_pass(accs[k, s], k, s, 1)
             nc.scalar.activation(tanhs[k][:, s * BANK : (s + 1) * BANK], accs[k, s][:], TANH)
             if s == 1:
-                if k < PACK:
-                    nc.vector.tensor_tensor(picked0[:, k, :], tanhs[k][:].indirect(pos_t[:]), gain0[:, k, :], MULT)
-                else:
-                    nc.vector.tensor_tensor(
-                        picked1[:, k - PACK, :], tanhs[k][:].indirect(pos_t[:, 0:16]), gain1[:, k - PACK, :], MULT
-                    )
-                if k == PACK - 1:
-                    woven0 = weave(picked0, 0, M2, "woven0")
+                pick(k, halves[0] if k == TILES - 1 else slice(0, M2))
                 if k == PACK:
-                    quantise_x(woven0, 0, slice(0, M2))
+                    woven = weave(nc.vector.tensor_copy, 0, 0)
+                if k == PACK + 1:
+                    quantise_x(woven, 0, 0)
 
         wgo_t = held.tile([P, PACK, M2], F32, name="wgo_t", tag="w4_wgo", align_bytes=64)
         for quad in range(4):
@@ -189,14 +195,17 @@ def tile_list_tarnish_patch_features_kernel(
 
         def round_w2(pair):
             c, t0 = pair // 2, 2 * (pair % 2)
-            tag = "first" if pair == 0 else f"rounded{pair}"
-            rounded = held.tile([P, PASSES, 2, P, PACK], BF16, name=f"w2_rounded{pair}", tag=tag, align_bytes=64)
+            if pair == 0:
+                flat = first_rounded
+            else:
+                flat = ring.tile([P, PASSES * 2 * P * PACK], BF16, name="w2_rounded", align_bytes=64)[:]
+            rounded = flat.rearrange("p (b t q j) -> p b t q j", b=PASSES, t=2, j=PACK)
             for b in range(PASSES):
                 nc.scalar.copy(
                     rounded[:, b, :, :, :].rearrange("p t q j -> p q j t"),
                     w2_raw[c][:, b, :, :].rearrange("p j (q t) -> p q j t", t=PACK)[:, :, :, t0 : t0 + 2],
                 )
-            return rounded
+            return flat
 
         def quantise_w2(rounded):
             codes = ring.tile([P, PASSES, 2, P], U32, name="w2_codes", align_bytes=64)
@@ -204,7 +213,7 @@ def tile_list_tarnish_patch_features_kernel(
             nc.vector.quantize_mx(
                 codes[:].rearrange("p b t q -> p (b t q)").bitcast(FP8X4),
                 scales[:].rearrange("p b t q -> p (b t q)"),
-                rounded[:].rearrange("p b t q j -> p (b t q j)"),
+                rounded,
             )
             return codes, scales
 
@@ -234,24 +243,21 @@ def tile_list_tarnish_patch_features_kernel(
             nc.vector.tensor_tensor(page[:].indirect(offsets), y[:, cols], wgo_t[:, k % PACK, cols], MULT)
 
         out_rows = out.rearrange("(b p t) j -> b t p j", b=PASSES, t=PACK)
-        halves = [slice(0, HALF), slice(HALF, M2)]
 
         rounded = round_w2(0)
-        woven1a = weave(picked1, 1, HALF, "woven1a")
+        late_woven = weave(nc.scalar.copy, 0, 1)
+        woven = weave(nc.vector.tensor_copy, 1, 0)
         weights = quantise_w2(rounded)
-        quantise_x(woven1a, 1, halves[0])
+        quantise_x(woven, 1, 0)
         page = make_page(0)
         y = ys.tile([P, M2], F32, name="y")
         second_stage(0, weights, y, halves[0])
         rounded = round_w2(1)
 
-        picked1 = held.tile([P, PACK, HALF], F32, name="picked1b", tag="first", align_bytes=64)
-        for t in range(PACK):
-            nc.vector.tensor_tensor(
-                picked1[:, t, :], tanhs[PACK + t][:].indirect(pos_t[:, 16:32]), gain1[:, t, :], MULT
-            )
-        woven1b = weave(picked1, 1, HALF, "woven1b")
-        quantise_x(woven1b, 1, halves[1])
+        pick(TILES - 1, halves[1])
+        quantise_x(late_woven, 0, 1)
+        woven = weave(nc.vector.tensor_copy, 1, 1)
+        quantise_x(woven, 1, 1)
         put(0, page, y, halves[0])
         second_stage(0, weights, y, halves[1])
         next_weights = quantise_w2(rounded)

@@ -22,7 +22,7 @@ PACK = 4
 PASSES = 2
 BANK = 512
 TILES = H // P
-BANKS = 4
+BANKS = 8
 HALF = M2 // 2
 
 
@@ -55,24 +55,23 @@ def tile_list_tarnish_patch_features_kernel(
         ]
         nc.sync.dma_start(w4_sc[0:32, :].bitcast(I32), w4_scales.rearrange("a q c -> q a c").bitcast(I32))
         nc.sync.dma_start(tab_sc[0:32, :].bitcast(I32), tab_scales.rearrange("a q t -> q a t").bitcast(I32))
+        vecs = {}
+        for name, vec, queue in (("gain", gain, nc.sync), ("skip", skip, nc.gpsimd), ("d", d, nc.gpsimd)):
+            vt = held.tile([P, PASSES, PACK], F32, name=f"{name}_t")
+            queue.dma_start(vt[:], vec.rearrange("(b p t) -> p b t", b=PASSES, t=PACK))
+            vecs[name] = vt[:].rearrange("p b t -> p (b t)")
         table = []
 
-        def load_table(a, piece):
+        def load_table(a):
             tab = held.tile([P, T], I32, name=f"table{a}", tag=f"big{a}", align_bytes=64)
-            nc.sync.dma_start(tab[:], tab_words[a].rearrange("p t i -> p (t i)").bitcast(I32), max_dma_last_dim=piece)
+            nc.sync.dma_start(tab[:], tab_words[a].rearrange("p t i -> p (t i)").bitcast(I32))
             table.append(tab)
 
         nc.sync.dma_start(w4_raw[0][:], w4_cols[0].bitcast(I32))
-        load_table(0, 4 * T)
+        load_table(0)
+        load_table(1)
         nc.sync.dma_start(pos_t[:], pos1)
-        load_table(1, T)
         nc.sync.dma_start(w4_raw[1][:], w4_cols[1].bitcast(I32))
-
-        vecs = {}
-        for name, vec in (("gain", gain), ("skip", skip), ("d", d)):
-            vt = held.tile([P, PASSES, PACK], F32, name=f"{name}_t")
-            nc.gpsimd.dma_start(vt[:], vec.rearrange("(b p t) -> p b t", b=PASSES, t=PACK))
-            vecs[name] = vt[:].rearrange("p b t -> p (b t)")
 
         rows = held.tile([P, S + H], U8, name="rows", align_bytes=64)
         nc.vector.tensor_copy(
@@ -102,15 +101,18 @@ def tile_list_tarnish_patch_features_kernel(
         page_scale = held.tile([P, TILES], F32, name="page_scale")
         nc.gpsimd.tensor_tensor(page_scale[:], vecs["gain"], vecs["skip"], MULT)
 
-        gains = held.tile([P, TILES, M2], F32, name="gains", tag="raw0", align_bytes=64)
-        nc.vector.tensor_copy(gains[:], vecs["gain"].unsqueeze(2).to_broadcast([P, TILES, M2]))
+        gains = []
+        for b, tag in enumerate(("gains0", "raw0")):
+            spread = held.tile([P, PACK, M2], F32, name=f"gains{b}", tag=tag, align_bytes=64)
+            nc.scalar.copy(spread[:], vecs["gain"][:, b * PACK : (b + 1) * PACK].unsqueeze(2).to_broadcast([P, PACK, M2]))
+            gains.append(spread)
 
         v_words = [held.tile([P, S], U32, name=f"v_words{a}", align_bytes=64) for a in range(PASSES)]
         nc.vector.tensor_copy(v_words[0][:], table[0][:].bitcast(U32).indirect(offs_t[:]))
 
-        groups = [(0, 0), (1, 0), (0, 1), (1, 1)] + [(k, s) for k in range(2, TILES) for s in range(2)]
+        groups = [(k, s) for k in range(TILES) for s in range(2)]
 
-        def first_stage_pass(acc, k, s, a):
+        def first_stage_pass(acc, k, s, a, opens):
             cols = slice(s * BANK, (s + 1) * BANK)
             first = a * BANK + (k % PACK) * P
             nc.tensor.matmul_mx(
@@ -119,14 +121,10 @@ def tile_list_tarnish_patch_features_kernel(
                 lhsT_scale=planes[:, a, S + k * P : S + (k + 1) * P],
                 rhs=v_words[a][:, cols].bitcast(FP8X4),
                 rhs_scale=planes[:, a, cols],
-                start=(a == 0),
-                stop=(a == PASSES - 1),
+                start=opens,
+                stop=not opens,
             )
 
-        accs = {}
-        for k, s in groups[:BANKS]:
-            accs[k, s] = psum.tile([P, BANK], F32, name="acc")
-            first_stage_pass(accs[k, s], k, s, 0)
         for s in range(2):
             nc.vector.tensor_copy(
                 v_words[1][:, s * BANK : (s + 1) * BANK],
@@ -172,16 +170,16 @@ def tile_list_tarnish_patch_features_kernel(
         def pick(k, cols):
             offsets = pos_t[:, cols.start // 16 : cols.stop // 16]
             nc.vector.tensor_tensor(
-                picked[k // PACK][:, k % PACK, cols], tanhs[k][:].indirect(offsets), gains[:, k, cols], MULT
+                picked[k // PACK][:, k % PACK, cols], tanhs[k][:].indirect(offsets), gains[k // PACK][:, k % PACK, cols], MULT
             )
 
         woven = None
         for k, s in groups:
-            if (k, s) not in accs:
-                accs[k, s] = psum.tile([P, BANK], F32, name="acc")
-                first_stage_pass(accs[k, s], k, s, 0)
-            first_stage_pass(accs[k, s], k, s, 1)
-            nc.scalar.activation(tanhs[k][:, s * BANK : (s + 1) * BANK], accs[k, s][:], TANH)
+            acc = psum.tile([P, BANK], F32, name="acc")
+            opener = 0 if k == 0 else 1
+            first_stage_pass(acc, k, s, opener, True)
+            first_stage_pass(acc, k, s, 1 - opener, False)
+            nc.scalar.activation(tanhs[k][:, s * BANK : (s + 1) * BANK], acc[:], TANH)
             if s == 1:
                 pick(k, halves[0] if k == TILES - 1 else slice(0, M2))
                 if k == PACK:

from contextlib import ExitStack

import concourse.mybir as mybir

K, T, S, H, M2 = 1024, 4096, 1024, 1024, 512
FLOPS = 2 * K * H * S + 2 * H * H * M2

F32 = mybir.dt.float32
BF16 = mybir.dt.bfloat16
I32 = mybir.dt.int32
U32 = mybir.dt.uint32
U16 = mybir.dt.uint16
U8 = mybir.dt.uint8
FP8X4 = mybir.dt.float8_e4m3fn_x4
FP4X4 = mybir.dt.float4_e2m1fn_x4
MULT = mybir.AluOpType.mult
TANH = mybir.ActivationFunctionType.Tanh
COPY = mybir.ActivationFunctionType.Copy

P = 128
PACK = 4
PASSES = 2
BANK = 512
TILES = H // P
BANKS = 8
HALF = M2 // 2


def tile_list_tarnish_patch_features_kernel(
    tc, tab_words, tab_scales, offs, pos1, w4_words, w4_scales, gain, w2, d, skip, wgo, out
):
    nc = tc.nc
    with ExitStack() as ctx:
        lists = ctx.enter_context(tc.tile_pool(name="lists", bufs=1))
        held = ctx.enter_context(tc.tile_pool(name="held", bufs=1))
        ring = ctx.enter_context(tc.tile_pool(name="ring", bufs=2))
        ys = ctx.enter_context(tc.tile_pool(name="ys", bufs=3))
        psum = ctx.enter_context(tc.psum_pool(name="psum", bufs=BANKS))

        offs_t = lists.tile([P, S // 16], U16, name="offs_t")
        pos_t = lists.tile([P, M2 // 16], U16, name="pos_t")
        nc.sync.dma_start(offs_t[:], offs)

        w4_sc = held.tile([P, H], U8, name="w4_sc", align_bytes=64)
        tab_sc = held.tile([P, T], U8, name="tab_sc", tag="early", align_bytes=64)
        planes = held.tile([P, PASSES, S + H], U8, name="planes", align_bytes=64)
        for lo, hi in ((32, 64), (64, P)):
            nc.vector.memset(w4_sc[lo:hi, :].bitcast(I32), 0)
            nc.vector.memset(tab_sc[lo:hi, :].bitcast(I32), 0)
        nc.vector.memset(planes[:].bitcast(I32), 0)
        w4_cols = w4_words.rearrange("a p (b c) -> b p a c", b=PASSES)
        w4_raw = [
            held.tile([P, PASSES, BANK // 2], I32, name=f"w4_raw{b}", tag=f"raw{b}", align_bytes=64)
            for b in range(PASSES)
        ]
        nc.sync.dma_start(w4_sc[0:32, :].bitcast(I32), w4_scales.rearrange("a q c -> q a c").bitcast(I32))
        nc.sync.dma_start(tab_sc[0:32, :].bitcast(I32), tab_scales.rearrange("a q t -> q a t").bitcast(I32))
        vecs = {}
        for name, vec, queue in (("gain", gain, nc.sync), ("skip", skip, nc.gpsimd), ("d", d, nc.gpsimd)):
            vt = held.tile([P, PASSES, PACK], F32, name=f"{name}_t")
            queue.dma_start(vt[:], vec.rearrange("(b p t) -> p b t", b=PASSES, t=PACK))
            vecs[name] = vt[:].rearrange("p b t -> p (b t)")
        table = []

        def load_table(a):
            tab = held.tile([P, T], I32, name=f"table{a}", tag=f"big{a}", align_bytes=64)
            nc.sync.dma_start(tab[:], tab_words[a].rearrange("p t i -> p (t i)").bitcast(I32))
            table.append(tab)

        nc.sync.dma_start(w4_raw[0][:], w4_cols[0].bitcast(I32))
        load_table(0)
        load_table(1)
        nc.sync.dma_start(pos_t[:], pos1)
        nc.sync.dma_start(w4_raw[1][:], w4_cols[1].bitcast(I32))

        rows = held.tile([P, S + H], U8, name="rows", align_bytes=64)
        nc.vector.tensor_copy(
            rows[:, S:].rearrange("p (b t q) -> p b t q", b=PASSES, t=PACK),
            w4_sc[:].rearrange("p (b q t) -> p b t q", b=PASSES, t=PACK),
        )
        v_sc = held.tile([P, S], U8, name="v_sc", align_bytes=64)
        nc.vector.tensor_copy(v_sc[:], tab_sc[:].indirect(offs_t[:]))
        nc.vector.tensor_copy(rows[:, :S].bitcast(I32), v_sc[:].bitcast(I32))
        for quad in range(4):
            nc.scalar.dma_start(
                planes[32 * quad : 32 * quad + 4, :, :].bitcast(I32),
                rows[8 * quad : 8 * quad + 8, :].bitcast(I32),
            )

        w4_dealt = []

        def deal_w4(b, tag):
            dealt = held.tile([P, PASSES * BANK * 2], U8, name=f"w4_dealt{b}", tag=tag, align_bytes=64)
            nc.vector.tensor_copy(
                dealt[:].bitcast(U16).rearrange("p (a t q) -> p a t q", t=PACK, q=P),
                w4_raw[b][:].rearrange("p a c -> p (a c)").bitcast(U16).rearrange("p (a q t) -> p a t q", t=PACK, q=P),
            )
            w4_dealt.append(dealt)

        deal_w4(0, "early")
        page_scale = held.tile([P, TILES], F32, name="page_scale")
        nc.gpsimd.tensor_tensor(page_scale[:], vecs["gain"], vecs["skip"], MULT)

        gains = []
        for b, tag in enumerate(("gains0", "raw0")):
            spread = held.tile([P, PACK, M2], F32, name=f"gains{b}", tag=tag, align_bytes=64)
            nc.scalar.copy(spread[:], vecs["gain"][:, b * PACK : (b + 1) * PACK].unsqueeze(2).to_broadcast([P, PACK, M2]))
            gains.append(spread)

        v_words = [held.tile([P, S], U32, name=f"v_words{a}", align_bytes=64) for a in range(PASSES)]
        nc.vector.tensor_copy(v_words[0][:], table[0][:].bitcast(U32).indirect(offs_t[:]))

        groups = [(k, s) for k in range(TILES) for s in range(2)]

        def first_stage_pass(acc, k, s, a, opens):
            cols = slice(s * BANK, (s + 1) * BANK)
            first = a * BANK + (k % PACK) * P
            nc.tensor.matmul_mx(
                acc[:],
                lhsT=w4_dealt[k // PACK][:, 2 * first : 2 * (first + P)].bitcast(FP4X4),
                lhsT_scale=planes[:, a, S + k * P : S + (k + 1) * P],
                rhs=v_words[a][:, cols].bitcast(FP8X4),
                rhs_scale=planes[:, a, cols],
                start=opens,
                stop=not opens,
            )

        for s in range(2):
            nc.vector.tensor_copy(
                v_words[1][:, s * BANK : (s + 1) * BANK],
                table[1][:].bitcast(U32).indirect(offs_t[:, s * 32 : (s + 1) * 32]),
            )

        deal_w4(1, "w4_wgo")

        w2_raw = []
        w2_rows = w2.rearrange("(b p j) n -> b p j n", b=PASSES, j=PACK)
        for c in range(2):
            raw = held.tile([P, PASSES, PACK, BANK], F32, name=f"w2_raw{c}", tag=f"big{c}", align_bytes=64)
            for b in range(PASSES):
                nc.sync.dma_start(raw[:, b, :, :], w2_rows[b][:, :, c * BANK : (c + 1) * BANK])
            w2_raw.append(raw)

        tanhs = [held.tile([P, S], F32, name=f"tanh{k}") for k in range(TILES)]
        x_codes = [held.tile([P, M2], U32, name=f"x_codes{b}", align_bytes=64) for b in range(PASSES)]
        x_scales = [held.tile([P, M2], U8, name=f"x_scales{b}", align_bytes=64) for b in range(PASSES)]

        def weave(copy, b, half):
            woven = held.tile([P, HALF, PACK], BF16, name=f"woven{b}{half}", align_bytes=64)
            copy(
                woven[:].rearrange("p (c i) t -> p c t i", i=4),
                picked[b][:, :, halves[half]].rearrange("p t (c i) -> p c t i", i=4),
            )
            return woven

        def quantise_x(woven, b, half):
            cols = halves[half]
            nc.vector.quantize_mx(
                x_codes[b][:, cols].bitcast(FP8X4),
                x_scales[b][:, cols],
                woven[:].rearrange("p m t -> p (m t)"),
            )

        halves = [slice(0, HALF), slice(HALF, M2)]
        picked0 = held.tile([P, PACK * M2], F32, name="picked0")
        shared = held.tile([P, PACK * M2 + 3 * HALF], F32, name="shared", align_bytes=64)
        picked = [flat.rearrange("p (t m) -> p t m", t=PACK) for flat in (picked0[:], shared[:, : PACK * M2])]
        first_rounded = shared[:, PACK * M2 - HALF :].bitcast(BF16)

        def pick(k, cols):
            offsets = pos_t[:, cols.start // 16 : cols.stop // 16]
            nc.vector.tensor_tensor(
                picked[k // PACK][:, k % PACK, cols], tanhs[k][:].indirect(offsets), gains[k // PACK][:, k % PACK, cols], MULT
            )

        woven = None
        for k, s in groups:
            acc = psum.tile([P, BANK], F32, name="acc")
            opener = 0 if k == 0 else 1
            first_stage_pass(acc, k, s, opener, True)
            first_stage_pass(acc, k, s, 1 - opener, False)
            nc.scalar.activation(tanhs[k][:, s * BANK : (s + 1) * BANK], acc[:], TANH)
            if s == 1:
                pick(k, halves[0] if k == TILES - 1 else slice(0, M2))
                if k == PACK:
                    woven = weave(nc.vector.tensor_copy, 0, 0)
                if k == PACK + 1:
                    quantise_x(woven, 0, 0)

        wgo_t = held.tile([P, PACK, M2], F32, name="wgo_t", tag="w4_wgo", align_bytes=64)
        for quad in range(4):
            nc.sync.dma_start(wgo_t[32 * quad : 32 * quad + 32, :, :], wgo.rearrange("(v t) m -> v t m", t=PACK))

        def round_w2(pair):
            c, t0 = pair // 2, 2 * (pair % 2)
            if pair == 0:
                flat = first_rounded
            else:
                flat = ring.tile([P, PASSES * 2 * P * PACK], BF16, name="w2_rounded", align_bytes=64)[:]
            rounded = flat.rearrange("p (b t q j) -> p b t q j", b=PASSES, t=2, j=PACK)
            for b in range(PASSES):
                nc.scalar.copy(
                    rounded[:, b, :, :, :].rearrange("p t q j -> p q j t"),
                    w2_raw[c][:, b, :, :].rearrange("p j (q t) -> p q j t", t=PACK)[:, :, :, t0 : t0 + 2],
                )
            return flat

        def quantise_w2(rounded):
            codes = ring.tile([P, PASSES, 2, P], U32, name="w2_codes", align_bytes=64)
            scales = ring.tile([P, PASSES, 2, P], U8, name="w2_scales", align_bytes=64)
            nc.vector.quantize_mx(
                codes[:].rearrange("p b t q -> p (b t q)").bitcast(FP8X4),
                scales[:].rearrange("p b t q -> p (b t q)"),
                rounded,
            )
            return codes, scales

        def second_stage(k, weights, y, cols):
            codes, scales = weights
            width = cols.stop - cols.start
            acc = psum.tile([P, BANK], F32, name="acc")
            for b in range(PASSES):
                nc.tensor.matmul_mx(
                    acc[:, :width],
                    lhsT=codes[:, b, k % 2, :].bitcast(FP8X4),
                    lhsT_scale=scales[:, b, k % 2, :],
                    rhs=x_codes[b][:, cols].bitcast(FP8X4),
                    rhs_scale=x_scales[b][:, cols],
                    start=(b == 0),
                    stop=(b == PASSES - 1),
                )
            nc.scalar.activation(y[:, cols], acc[:, :width], TANH, bias=vecs["d"][:, k : k + 1])

        def make_page(k):
            page = held.tile([P, S], F32, name=f"page{k}")
            nc.scalar.activation(page[:], tanhs[k][:], COPY, scale=page_scale[:, k : k + 1])
            return page

        def put(k, page, y, cols):
            offsets = pos_t[:, cols.start // 16 : cols.stop // 16]
            nc.vector.tensor_tensor(page[:].indirect(offsets), y[:, cols], wgo_t[:, k % PACK, cols], MULT)

        out_rows = out.rearrange("(b p t) j -> b t p j", b=PASSES, t=PACK)

        rounded = round_w2(0)
        late_woven = weave(nc.scalar.copy, 0, 1)
        woven = weave(nc.vector.tensor_copy, 1, 0)
        weights = quantise_w2(rounded)
        quantise_x(woven, 1, 0)
        page = make_page(0)
        y = ys.tile([P, M2], F32, name="y")
        second_stage(0, weights, y, halves[0])
        rounded = round_w2(1)

        pick(TILES - 1, halves[1])
        quantise_x(late_woven, 0, 1)
        woven = weave(nc.vector.tensor_copy, 1, 1)
        quantise_x(woven, 1, 1)
        put(0, page, y, halves[0])
        second_stage(0, weights, y, halves[1])
        next_weights = quantise_w2(rounded)
        put(0, page, y, halves[1])
        nc.sync.dma_start(out_rows[0][0], page[:])

        for k in range(1, TILES):
            if k % 2 == 0:
                weights = next_weights
            page = make_page(k)
            y = ys.tile([P, M2], F32, name="y")
            second_stage(k, weights, y, slice(0, M2))
            put(k, page, y, slice(0, M2))
            nc.sync.dma_start(out_rows[k // PACK][k % PACK], page[:])
            if k % 2 == 0 and k + 2 < TILES:
                next_weights = quantise_w2(round_w2(k // 2 + 1))
